import numpy as np
import ml_dtypes


def mxq(x, axis, fmt="e4m3"):
    dtype, down = {"e4m3": (ml_dtypes.float8_e4m3fn, 7), "e5m2": (ml_dtypes.float8_e5m2, 14)}[fmt]
    v = np.moveaxis(np.asarray(x, np.float32).astype(ml_dtypes.bfloat16).astype(np.float64), axis, -1)
    blocks = v.reshape(v.shape[:-1] + (-1, 32))
    amax = np.abs(blocks).max(-1, keepdims=True)
    byte = np.maximum(np.where(amax > 0, np.frexp(amax)[1] - 1 + 127, 0) - down, 1)
    scale = np.exp2(byte - 127.0)
    codes = (blocks / scale).astype(np.float32).astype(dtype).astype(np.float64)
    return np.moveaxis((codes * scale).reshape(v.shape), -1, axis)


WIDE = False


def mx_kscale(k):
    if not WIDE:
        return np.ones(k)
    levels = np.array([10, -10, 5, -5, 0])
    if k % 512:
        return np.exp2(np.random.permutation(np.resize(levels, k // 32))).repeat(32)
    a = np.empty((k // 512, 16))
    for p in range(k // 512):
        a[p, :8] = np.random.permutation(np.resize(levels, 8))
        for g in range(8):
            far = levels[np.abs(levels - a[p, g]) >= 10]
            a[p, g + 8] = far[np.random.randint(len(far))]
    return np.exp2(a.ravel()).repeat(32)


def f64(x):
    return np.asarray(x).astype(np.float64)


def striped(idx):
    return np.tile(idx.reshape(-1, 16).T, (8, 1)).astype(np.uint16)


def unstriped(offs):
    return offs[:16].T.reshape(-1).astype(np.int64)


E2M1 = np.array([0.0, 0.5, 1.0, 1.5, 2.0, 3.0, 4.0, 6.0, -0.0, -0.5, -1.0, -1.5, -2.0, -3.0, -4.0, -6.0])


def pack_weight(w, fmt):
    k, n = w.shape
    w = f64(np.asarray(w, np.float32).astype(ml_dtypes.bfloat16)).reshape(k // 32, 32, n)
    amax = np.abs(w).max(1)
    if fmt == "e4m3":
        byte = np.frexp(amax)[1] - 1 + 127 - 7
    else:
        mant, ex = np.frexp(amax / 6.0)
        byte = np.where(mant > 0.5, ex, ex - 1) + 127
    byte = np.clip(np.where(amax > 0, byte, 1), 1, 254)
    scaled = (w * np.exp2(127.0 - byte)[:, None, :]).reshape(k, n).astype(np.float32)
    by_word = np.ascontiguousarray(scaled.reshape(k // 512, 128, 4, n).transpose(0, 1, 3, 2))
    if fmt == "e4m3":
        words = by_word.astype(ml_dtypes.float8_e4m3fn).view(np.uint8)
    else:
        c = by_word.astype(ml_dtypes.float4_e2m1fn).view(np.uint8) & 0xF
        words = (c[..., 0::2] | (c[..., 1::2] << 4)).reshape(k // 512, 128, 2 * n)
    return np.ascontiguousarray(words), np.ascontiguousarray(byte.astype(np.uint8).reshape(k // 512, 16, n))


def unpack_weight(words, scales, fmt):
    g, _, n = scales.shape
    words = np.ascontiguousarray(words).reshape(g, 128, n, -1)
    if fmt == "e4m3":
        vals = words.view(ml_dtypes.float8_e4m3fn).astype(np.float64)
    else:
        nib = np.empty((g, 128, n, 4), np.uint8)
        nib[..., 0::2] = words & 0xF
        nib[..., 1::2] = words >> 4
        vals = E2M1[nib]
    vals = vals * np.repeat(np.exp2(scales.astype(np.float64) - 127.0), 8, axis=1)[..., None]
    return vals.transpose(0, 1, 3, 2).reshape(g * 512, n)


def gelu(v):
    return 0.5 * v * (1.0 + np.tanh(np.sqrt(2.0 / np.pi) * (v + 0.044715 * v**3)))


K, K2, T, T3, S, H, T2, P, N = 1024, 512, 2048, 1024, 512, 1024, 2048, 1024, 512

def setup_inputs():
    n = np.random.standard_normal
    s, s2, u = mx_kscale(K)[:, None], mx_kscale(K2)[:, None], mx_kscale(H)[:, None]
    d = {}
    d["tab_words"], d["tab_scales"] = pack_weight(n((K, T)) * s, "e4m3")
    d["tab2_words"], d["tab2_scales"] = pack_weight(n((K2, T3)) * s2, "e4m3")
    d["offs"] = striped(np.random.permutation(T)[:S])
    d["offs2"] = striped(np.random.permutation(T3)[:S])
    perm = np.random.permutation(T2)
    d["offs3"] = striped(perm[:S])
    d["offs4"] = striped(perm[S:2 * S])
    d["offs5"] = striped(np.random.permutation(T2)[:P])
    d["w1"] = (1.5 * n((K, H)) / s / K**0.5).astype(np.float32)
    d["w2_words"], d["w2_scales"] = pack_weight(0.8 * n((K, H)) / s / K**0.5, "e4m3")
    d["w3"] = (1.5 * n((K2, H)) / s2 / K2**0.5).astype(np.float32)
    d["w4_words"], d["w4_scales"] = pack_weight(n((H, N)) / u / H**0.5, "e2m1")
    d["wg1"] = np.exp(0.3 * n((128, S))).astype(np.float32)
    d["wg2"] = np.exp(0.3 * n((128, S))).astype(np.float32)
    d["page0"] = n((H, T2)).astype(np.float32)
    d["mid"] = (0.7 * n(H)).astype(np.float32)
    d["gn"] = (np.exp(0.3 * n(H)) * u[:, 0]).astype(np.float32)
    return d

def reference(tab_words, tab_scales, tab2_words, tab2_scales, offs, offs2, offs3, offs4, offs5, w1, w2_words, w2_scales, w3, w4_words, w4_scales, wg1, wg2, page0, mid, gn):
    v = unpack_weight(tab_words, tab_scales, "e4m3")[:, unstriped(offs)]
    v2 = unpack_weight(tab2_words, tab2_scales, "e4m3")[:, unstriped(offs2)]
    w2 = unpack_weight(w2_words, w2_scales, "e4m3")
    w4 = unpack_weight(w4_words, w4_scales, "e2m1")
    h1 = np.tanh(mxq(f64(w1), 0, "e4m3").T @ v) + (w2.T @ v)
    h2 = np.exp(np.tanh(mxq(f64(w3), 0, "e4m3").T @ v2))
    page = f64(page0).copy()
    page[:, unstriped(offs3)] = np.tile(f64(wg1), (H // 128, 1)) * h1
    page[:, unstriped(offs4)] = np.tile(f64(wg2), (H // 128, 1)) * h2
    x = (page[:, unstriped(offs5)] - f64(mid)[:, None]) * f64(gn)[:, None]
    y = w4.T @ mxq(x, 0, "e4m3")
    return np.square(y)

@@ -1,0 +1,384 @@
+from contextlib import ExitStack
+
+import concourse.mybir as mybir
+from concourse.masks import make_identity
+
+K, K2, T, T3, S, H, T2, PICKS, N = 1024, 512, 2048, 1024, 512, 1024, 2048, 1024, 512
+FLOPS = 2 * (2 * K * H * S + K2 * H * S + H * N * PICKS)
+
+F32 = mybir.dt.float32
+BF16 = mybir.dt.bfloat16
+I32 = mybir.dt.int32
+U32 = mybir.dt.uint32
+U16 = mybir.dt.uint16
+U8 = mybir.dt.uint8
+FP8X4 = mybir.dt.float8_e4m3fn_x4
+FP4X4 = mybir.dt.float4_e2m1fn_x4
+ACT = mybir.ActivationFunctionType
+ALU = mybir.AluOpType
+
+P = 128
+CHUNK = 256
+PLANE_ORDER = (2, 0, 1, 3)
+
+
+def tile_list_annuity_slot_features_kernel(
+    tc, tab_words, tab_scales, tab2_words, tab2_scales, offs, offs2, offs3, offs4, offs5,
+    w1, w2_words, w2_scales, w3, w4_words, w4_scales, wg1, wg2, page0, mid, gn, out,
+):
+    nc = tc.nc
+    with ExitStack() as ctx:
+        keep = ctx.enter_context(tc.tile_pool(name="keep", bufs=1))
+        psum = ctx.enter_context(tc.psum_pool(name="psum", bufs=1))
+
+        def sb(name, shape, dtype):
+            return keep.tile(shape, dtype, name=name, align_bytes=64)
+
+        lists = {}
+        for name, src in (("offs", offs), ("offs2", offs2), ("offs3", offs3), ("offs4", offs4), ("offs5", offs5)):
+            lists[name] = (keep.tile(list(src.shape), U16, name="l_" + name), src)
+
+        def load_list(name):
+            nc.sync.dma_start(lists[name][0][:], lists[name][1])
+
+        idx, idx2, idx3, idx4, idx5 = (lists[n][0] for n in ("offs", "offs2", "offs3", "offs4", "offs5"))
+
+        banks = [psum.tile([P, 512], F32, name="bank%d" % b) for b in range(8)]
+        pages = [sb("page%d" % t, [P, T2], F32) for t in range(8)]
+        tabw = [sb("tabw%d" % a, [P, T], I32) for a in range(2)]
+        tabs = sb("tabs", [P, T], U8)
+        tab2w = sb("tab2w", [P, T3], I32)
+        tab2s = sb("tab2s", [P, T3], U8)
+        vw = [sb("vw%d" % a, [P, S], U32) for a in range(2)]
+        vs = sb("vs", [P, S], U8)
+        v2w = sb("v2w", [P, S], U32)
+        v2s = sb("v2s", [P, S], U8)
+        w1raw = [sb("w1raw%d" % a, [P, 2048], F32) for a in range(2)]
+        w3raw = sb("w3raw", [P, 2048], F32)
+        w3st = sb("w3st", [P, 2048], BF16)
+        joint = sb("joint", [P, PICKS + S], F32)
+        slots = [joint[:, 0:PICKS]] + [sb("slot%d" % s, [P, PICKS], F32)[:] for s in range(1, 4)]
+        w1q = [sb("w1q%d" % b, [P, 1024], U32) for b in range(2)]
+        w1s = [sb("w1s%d" % b, [P, 1024], U8) for b in range(2)]
+        w3q = [sb("w3q%d" % b, [P, 512], U32) for b in range(2)]
+        w3s = [sb("w3s%d" % b, [P, 512], U8) for b in range(2)]
+        w2lo = [sb("w2lo%d" % u, [P, 2, 256], I32) for u in range(2)]
+        w2hi = sb("w2hi", [P, 2, 512], I32)
+        w2s = sb("w2s", [P, H], U8)
+        w4w = sb("w4w", [P, 2, 2 * N], U8)
+        w4s = sb("w4s", [P, 2, N], U8)
+        wgn = [sb("wgn%d" % i, [P, S], F32) for i in range(2)]
+        wgp = [sb("wgp%d" % i, [P, 4, S], F32) for i in range(2)]
+        h1 = [joint[:, PICKS:] if s == 1 else sb("h1_%d" % s, [P, S], F32)[:] for s in range(4)]
+        h2 = [sb("h2_%d" % s, [P, S], F32) for s in range(4)]
+        tanh_t = [sb("tanh%d" % s, [P, 512], F32) for s in range(2)]
+        lin_t = [sb("lin%d" % s, [P, 512], F32) for s in range(2)]
+        lin1 = sb("lin_hi", [P, 2048], F32)
+        xq = [sb("xq%d" % b, [P, PICKS], U32) for b in range(2)]
+        xs = [sb("xs%d" % b, [P, PICKS], U8) for b in range(2)]
+        midc = [sb("mid%d" % b, [P, 4], F32) for b in range(2)]
+        gnc = [sb("gn%d" % b, [P, 4], F32) for b in range(2)]
+        shift = [sb("shift%d" % b, [P, 4], F32) for b in range(2)]
+        ident = sb("ident", [P, P], F32)
+        identb = sb("identb", [P, P], BF16)
+
+        def load_scale_rows(dst, src, passes):
+            for q in range(4):
+                nc.sync.dma_start(
+                    dst[32 * q : 32 * q + 4 * passes, :].bitcast(I32),
+                    src[:, 4 * q : 4 * q + 4, :].bitcast(I32),
+                )
+
+        def load_words(dst, src):
+            nc.sync.dma_start(dst[:], src.rearrange("p t i -> p (t i)").bitcast(I32))
+
+        def load_page(t):
+            b, s = divmod(t, 4)
+            rows = page0[512 * b : 512 * (b + 1), :]
+            if b == 0:
+                nc.sync.dma_start(pages[t][:], rows[P * s : P * (s + 1), :])
+            else:
+                nc.sync.dma_start(pages[t][:], rows.rearrange("(p i) c -> p i c", i=4)[:, s, :])
+
+        def load_weight(raw, w, a, c0, width):
+            start = 4 * (c0 % 512)
+            nc.sync.dma_start(
+                raw[:, start : start + 4 * width].rearrange("p (j c) -> p j c", j=4),
+                w[512 * a : 512 * (a + 1), c0 : c0 + width].rearrange("(p j) c -> p j c", j=4),
+            )
+
+        def load_w2(dst, c0, width):
+            src = w2_words.rearrange("a p c i -> p a (c i)")[:, :, 4 * c0 : 4 * (c0 + width)]
+            nc.sync.dma_start(dst[:], src.bitcast(I32))
+
+        def load_dealt_gates(dst, wg):
+            for q in range(4):
+                nc.sync.dma_start(dst[32 * q : 32 * (q + 1), :, :], wg.rearrange("(u i) s -> u i s", i=4))
+
+        def weave(copy, dst, src, dealt):
+            if dealt:
+                copy(dst.rearrange("p (t m j) -> p m j t", t=4, j=4), src.rearrange("p (j m t) -> p m j t", j=4, t=4))
+            else:
+                copy(dst.rearrange("p (c i j) -> p c j i", i=4, j=4), src.rearrange("p (j c i) -> p c j i", j=4, i=4))
+
+        def quantize(codes, scales, src):
+            nc.vector.quantize_mx(out=codes.bitcast(FP8X4), scales=scales, in_=src)
+
+        def stream2(t, bent, dst):
+            b, s = divmod(t, 4)
+            cols = slice(P * s, P * (s + 1))
+            bank = banks[5 * b]
+            nc.tensor.matmul_mx(
+                bank[:], lhsT=w3q[b][:, cols].bitcast(FP8X4), lhsT_scale=w3s[b][:, cols],
+                rhs=v2w[:].bitcast(FP8X4), rhs_scale=v2s[:], start=True, stop=True,
+            )
+            nc.scalar.activation(bent, bank[:], ACT.Tanh)
+            if dst is not None:
+                nc.scalar.activation(dst, bent, ACT.Exp)
+
+        def picked(a, jb):
+            cols = slice(P * jb, P * (jb + 1))
+            return dict(lhsT=vw[a][:, cols].bitcast(FP8X4), lhsT_scale=vs[4 * a : P, cols])
+
+        def linear_low(s):
+            bank = banks[4 + s % 2]
+            for jb in range(4):
+                for a in range(2):
+                    nc.tensor.matmul_mx(
+                        bank[:, P * jb : P * (jb + 1)], rhs=w2lo[s // 2][:, a, P * (s % 2) : P * (s % 2 + 1)].bitcast(FP8X4),
+                        rhs_scale=w2s[4 * a : P, P * s : P * (s + 1)], start=(a == 0), stop=(a == 1), **picked(a, jb),
+                    )
+            nc.scalar.copy(lin_t[s % 2][:], bank[:])
+
+        def linear_high():
+            for jb in range(4):
+                bank = banks[4 + jb % 2]
+                for a in range(2):
+                    nc.tensor.matmul_mx(
+                        bank[:], rhs=w2hi[:, a, :].bitcast(FP8X4), rhs_scale=w2s[4 * a : P, 512:1024],
+                        start=(a == 0), stop=(a == 1), **picked(a, jb),
+                    )
+                nc.scalar.copy(
+                    lin1[:].rearrange("p (i b m) -> p b i m", i=4, b=4)[:, jb, :, :],
+                    bank[:].rearrange("p (m i) -> p i m", i=4),
+                )
+
+        def stream1(t, step):
+            b, s = divmod(t, 4)
+            bank = banks[2 + step % 2]
+            for jb in range(4):
+                for a in range(2):
+                    c0 = 512 * (s // 2) + 256 * a + P * (s % 2) if b == 0 else 512 * a + P * s
+                    nc.tensor.matmul_mx(
+                        bank[:, P * jb : P * (jb + 1)], rhs=w1q[b][:, c0 : c0 + P].bitcast(FP8X4),
+                        rhs_scale=w1s[b][:, c0 : c0 + P], start=(a == 0), stop=(a == 1), **picked(a, jb),
+                    )
+            bent = tanh_t[step % 2]
+            nc.scalar.activation(bent[:], bank[:], ACT.Tanh)
+            lin = lin_t[s % 2][:] if b == 0 else lin1[:, 512 * s : 512 * (s + 1)]
+            total = banks[6 + step % 2]
+            for jb in range(4):
+                cols = slice(P * jb, P * (jb + 1))
+                nc.tensor.matmul(total[:, cols], lhsT=lin[:, cols], rhs=ident[:], is_transpose=True, start=True, stop=False)
+                nc.tensor.matmul(total[:, cols], lhsT=bent[:, cols], rhs=ident[:], is_transpose=True, start=False, stop=True)
+            if t not in (1, 7):
+                nc.scalar.copy(h1[step % 4][:], total[:])
+
+        def put(t, step, which, values=None):
+            b, s = divmod(t, 4)
+            gate = wgn[which][:] if b == 0 else wgp[which][:, s, :]
+            if values is None:
+                values = (h1, h2)[which][step % 4][:]
+            nc.vector.tensor_tensor(pages[t][:].indirect((idx3, idx4)[which][:]), values, gate, ALU.mult)
+
+        def fetch(t, slot):
+            nc.vector.tensor_copy(slot, pages[t][:].indirect(idx5[:]))
+
+        for plane in (tab2s, tabs, w2s):
+            nc.vector.memset(plane[:].bitcast(I32), 0)
+        nc.vector.memset(w4s[:].rearrange("p a c -> p (a c)").bitcast(I32), 0)
+        make_identity(nc, ident[:])
+        make_identity(nc, identb[:])
+
+        load_scale_rows(tab2s, tab2_scales, 1)
+        load_list("offs2")
+        load_weight(w3raw, w3, 0, 0, 256)
+        load_words(tab2w, tab2_words[0])
+        load_page(0)
+        nc.sync.dma_start(wgn[1][:], wg2)
+        load_list("offs4")
+
+        nc.vector.tensor_copy(v2s[:], tab2s[:].indirect(idx2[:]))
+        weave(nc.vector.tensor_copy, w3st[:, 0:1024], w3raw[:, 0:1024], False)
+        quantize(w3q[0][:, 0:256], w3s[0][:, 0:256], w3st[:, 0:1024])
+        nc.vector.tensor_copy(v2w[:], tab2w[:].bitcast(U32).indirect(idx2[:]))
+        stream2(0, h2[0][:], h2[0][:])
+        put(0, 0, 1)
+        stream2(1, h2[1][:], h2[1][:])
+
+        load_weight(w3raw, w3, 0, 256, 256)
+        load_page(1)
+        load_list("offs")
+        load_scale_rows(tabs, tab_scales, 2)
+        for a in range(2):
+            load_weight(w1raw[a], w1, a, 0, 256)
+        for a in range(2):
+            load_words(tabw[a], tab_words[a])
+        load_page(2)
+        load_scale_rows(w2s, w2_scales, 2)
+        load_w2(w2lo[0], 0, 256)
+        load_page(3)
+        nc.sync.dma_start(wgn[0][:], wg1)
+        load_list("offs3")
+        for a in range(2):
+            load_weight(w1raw[a], w1, a, 256, 256)
+        load_w2(w2lo[1], 256, 256)
+        load_list("offs5")
+
+        weave(nc.scalar.copy, w3st[:, 1024:2048], w3raw[:, 1024:2048], False)
+        quantize(w3q[0][:, 256:512], w3s[0][:, 256:512], w3st[:, 1024:2048])
+        stream2(2, h2[2][:], h2[2][:])
+        stream2(3, h2[3][:], h2[3][:])
+        put(1, 1, 1)
+
+        def low_pair(u, slot):
+            staged = slot[:].bitcast(BF16)
+            for a in range(2):
+                weave(nc.scalar.copy, staged[:, 1024 * a : 1024 * (a + 1)], w1raw[a][:, 1024 * u : 1024 * (u + 1)], False)
+            quantize(w1q[0][:, 512 * u : 512 * (u + 1)], w1s[0][:, 512 * u : 512 * (u + 1)], staged)
+
+        nc.vector.tensor_copy(vs[:], tabs[:].indirect(idx[:]))
+        low_pair(0, slots[1])
+        for a in range(2):
+            nc.vector.tensor_copy(vw[a][:], tabw[a][:].bitcast(U32).indirect(idx[:]))
+        for s in range(2):
+            linear_low(s)
+            stream1(s, s)
+        put(2, 2, 1)
+        put(3, 3, 1)
+        low_pair(1, joint[:, S:])
+        nc.scalar.copy(h1[1], banks[7][:])
+        put(0, 0, 0)
+        fetch(0, slots[0][:])
+        put(1, 1, 0)
+        for s in range(2, 4):
+            linear_low(s)
+            stream1(s, s)
+
+        with nc.allow_non_contiguous_dma(reason="one value a partition"):
+            for dst, src in ((midc, mid), (gnc, gn)):
+                nc.sync.dma_start(dst[0][:], src[0:512].rearrange("(s p) -> p s", p=P))
+                nc.sync.dma_start(dst[1][:], src[512:1024].rearrange("(p i) -> p i", i=4))
+        load_weight(w3raw, w3, 0, 512, 512)
+        load_w2(w2hi, 512, 512)
+        load_dealt_gates(wgp[1], wg2)
+        for a in (1, 0):
+            load_weight(w1raw[a], w1, a, 512, 512)
+        load_page(4 + PLANE_ORDER[0])
+        load_dealt_gates(wgp[0], wg1)
+        load_page(4 + PLANE_ORDER[1])
+        for q in range(4):
+            nc.sync.dma_start(
+                w4s[32 * q : 32 * q + 4, :, :].bitcast(I32),
+                w4_scales[:, 4 * q : 4 * q + 4, :].rearrange("a r c -> r a c").bitcast(I32),
+            )
+        nc.sync.dma_start(w4w[:].bitcast(I32), w4_words.rearrange("a p c -> p a c").bitcast(I32))
+        for s in PLANE_ORDER[2:]:
+            load_page(4 + s)
+
+        fetch(1, slots[1][:])
+        for b in range(2):
+            nc.vector.scalar_tensor_tensor(shift[b][:], midc[b][:], -1.0, gnc[b][:], ALU.mult, ALU.mult)
+
+        weave(nc.scalar.copy, w3st[:], w3raw[:], True)
+        quantize(w3q[1][:], w3s[1][:], w3st[:])
+        for a in (1, 0):
+            weave(nc.scalar.copy, slots[2 + a][:].bitcast(BF16), w1raw[a][:], True)
+        put(2, 2, 0)
+        put(3, 3, 0)
+        for a in (1, 0):
+            quantize(w1q[1][:, 512 * a : 512 * (a + 1)], w1s[1][:, 512 * a : 512 * (a + 1)], slots[2 + a][:].bitcast(BF16))
+        linear_high()
+        h2_high = [w1raw[0][:, S * step : S * (step + 1)] for step in range(4)]
+        for step, s in enumerate(PLANE_ORDER):
+            stream2(4 + s, h2_high[step], h2_high[step] if step < 3 else None)
+            stream1(4 + s, step)
+        fetch(2, slots[2][:])
+        fetch(3, slots[3][:])
+
+        xb = w1raw[1][:].bitcast(BF16)
+        for s in range(4):
+            nc.scalar.activation(
+                xb[:, PICKS * s : PICKS * (s + 1)], slots[s][:], ACT.Identity,
+                bias=shift[0][:, s : s + 1], scale=gnc[0][:, s : s + 1],
+            )
+        for g in range(4):
+            turned = banks[g % 2][:].bitcast(BF16)
+            for jj in range(2):
+                for s in range(4):
+                    j0 = PICKS * s + CHUNK * g + P * jj
+                    nc.tensor.transpose(turned[:, 512 * jj + P * s : 512 * jj + P * (s + 1)], xb[:, j0 : j0 + P], identb[:])
+            words = tanh_t[g % 2]
+            nc.scalar.copy(words[:].bitcast(BF16), turned)
+            back = banks[4 + g % 2]
+            for jj in range(2):
+                for u in range(2):
+                    c0 = 256 * jj + P * u
+                    nc.tensor.transpose(back[:, c0 : c0 + P], words[:, 256 * jj + u : 256 * (jj + 1) : 2], ident[:])
+            nc.scalar.copy(
+                lin1[:, 512 * g : 512 * (g + 1)].rearrange("p (b j u) -> p b j u", b=2, u=2),
+                back[:].rearrange("p (b u j) -> p b j u", b=2, u=2),
+            )
+
+        woven = xb.rearrange("p (j i) -> p j i", i=4)
+        for step, s in enumerate(PLANE_ORDER[:3]):
+            put(4 + s, step, 1, h2_high[step])
+            put(4 + s, step, 0)
+            slot = slots[step][:]
+            if step == 2:
+                quantize(xq[0][:], xs[0][:], lin1[:].bitcast(BF16))
+                slot = lin1[:, 0:PICKS]
+                nc.scalar.activation(lin1[:, 1024:1536], h2_high[3], ACT.Exp)
+                nc.scalar.copy(lin1[:, 1536:2048], banks[7][:])
+            fetch(4 + s, slot)
+            nc.scalar.activation(
+                woven[:, :, s], slot, ACT.Identity,
+                bias=shift[1][:, s : s + 1], scale=gnc[1][:, s : s + 1],
+            )
+        put(4 + PLANE_ORDER[3], 3, 1, lin1[:, 1024:1536])
+        put(4 + PLANE_ORDER[3], 3, 0, lin1[:, 1536:2048])
+
+        def last_product(b, c):
+            for half in range(2):
+                bank = banks[2 * c + half]
+                for nn in range(2):
+                    nt = 2 * half + nn
+                    for jj in range(2):
+                        j0 = CHUNK * c + P * jj
+                        nc.tensor.matmul_mx(
+                            bank[:, CHUNK * nn + P * jj : CHUNK * nn + P * (jj + 1)],
+                            lhsT=w4w[:, b, 2 * P * nt : 2 * P * (nt + 1)].bitcast(FP4X4),
+                            lhsT_scale=w4s[:, b, P * nt : P * (nt + 1)],
+                            rhs=xq[b][:, j0 : j0 + P].bitcast(FP8X4), rhs_scale=xs[b][:, j0 : j0 + P],
+                            start=(b == 0 and nn == 0 and jj == 0), stop=(b == 1 and nn == 1 and jj == 1),
+                        )
+                if b == 1:
+                    staged = (h2 + h1)[2 * c + half]
+                    nc.scalar.activation(staged[:], bank[:], ACT.Square)
+                    nc.sync.dma_start(
+                        out.rearrange("(n p) j -> p n j", p=P)[:, 2 * half : 2 * half + 2, CHUNK * c : CHUNK * (c + 1)],
+                        staged[:].rearrange("p (n j) -> p n j", n=2),
+                    )
+
+        for c in range(4):
+            last_product(0, c)
+        s = PLANE_ORDER[3]
+        for c in range(4):
+            cols = slice(CHUNK * c, CHUNK * (c + 1))
+            got = slots[0][:, CHUNK * (c % 2) : CHUNK * (c % 2 + 1)]
+            nc.vector.tensor_copy(got, pages[4 + s][:].indirect(idx5[:, 16 * c : 16 * (c + 1)]))
+            nc.vector.tensor_scalar(
+                woven[:, cols, s], got, midc[1][:, s : s + 1], gnc[1][:, s : s + 1], ALU.subtract, ALU.mult,
+            )
+            quantize(xq[1][:, cols], xs[1][:, cols], xb[:, 4 * CHUNK * c : 4 * CHUNK * (c + 1)])
+            last_product(1, c)

@@ -70,6 +70,9 @@ def tile_list_annuity_slot_features_kernel(
         wgn = [sb("wgn%d" % i, [P, S], F32) for i in range(2)]
         wgp = [sb("wgp%d" % i, [P, 4, S], F32) for i in range(2)]
         h1 = [joint[:, PICKS:] if s == 1 else sb("h1_%d" % s, [P, S], F32)[:] for s in range(4)]
+        pair_raw = [
+            [wgp[1 - u][:].rearrange("p i s -> p (i s)")[:, 1024 * a : 1024 * (a + 1)] for a in range(2)] for u in range(2)
+        ]
         h2 = [sb("h2_%d" % s, [P, S], F32) for s in range(4)]
         tanh_t = [sb("tanh%d" % s, [P, 512], F32) for s in range(2)]
         lin_t = [sb("lin%d" % s, [P, 512], F32) for s in range(2)]
@@ -82,9 +85,9 @@ def tile_list_annuity_slot_features_kernel(
         ident = sb("ident", [P, P], F32)
         identb = sb("identb", [P, P], BF16)
 
-        def load_scale_rows(dst, src, passes):
+        def load_scale_rows(queue, dst, src, passes):
             for q in range(4):
-                nc.sync.dma_start(
+                queue.dma_start(
                     dst[32 * q : 32 * q + 4 * passes, :].bitcast(I32),
                     src[:, 4 * q : 4 * q + 4, :].bitcast(I32),
                 )
@@ -101,9 +104,8 @@ def tile_list_annuity_slot_features_kernel(
                 nc.sync.dma_start(pages[t][:], rows.rearrange("(p i) c -> p i c", i=4)[:, s, :])
 
         def load_weight(raw, w, a, c0, width):
-            start = 4 * (c0 % 512)
             nc.sync.dma_start(
-                raw[:, start : start + 4 * width].rearrange("p (j c) -> p j c", j=4),
+                raw.rearrange("p (j c) -> p j c", j=4),
                 w[512 * a : 512 * (a + 1), c0 : c0 + width].rearrange("(p j) c -> p j c", j=4),
             )
 
@@ -124,10 +126,9 @@ def tile_list_annuity_slot_features_kernel(
         def quantize(codes, scales, src):
             nc.vector.quantize_mx(out=codes.bitcast(FP8X4), scales=scales, in_=src)
 
-        def stream2(t, bent, dst):
+        def stream2(t, bank, bent, dst):
             b, s = divmod(t, 4)
             cols = slice(P * s, P * (s + 1))
-            bank = banks[5 * b]
             nc.tensor.matmul_mx(
                 bank[:], lhsT=w3q[b][:, cols].bitcast(FP8X4), lhsT_scale=w3s[b][:, cols],
                 rhs=v2w[:].bitcast(FP8X4), rhs_scale=v2s[:], start=True, stop=True,
@@ -165,7 +166,7 @@ def tile_list_annuity_slot_features_kernel(
 
         def stream1(t, step):
             b, s = divmod(t, 4)
-            bank = banks[2 + step % 2]
+            bank = banks[2 + (step + b) % 2]
             for jb in range(4):
                 for a in range(2):
                     c0 = 512 * (s // 2) + 256 * a + P * (s % 2) if b == 0 else 512 * a + P * s
@@ -197,13 +198,16 @@ def tile_list_annuity_slot_features_kernel(
         for plane in (tab2s, tabs, w2s):
             nc.vector.memset(plane[:].bitcast(I32), 0)
         nc.vector.memset(w4s[:].rearrange("p a c -> p (a c)").bitcast(I32), 0)
+        load_scale_rows(nc.gpsimd, tabs, tab_scales, 2)
+        load_scale_rows(nc.gpsimd, w2s, w2_scales, 2)
         make_identity(nc, ident[:])
         make_identity(nc, identb[:])
 
-        load_scale_rows(tab2s, tab2_scales, 1)
+        load_scale_rows(nc.sync, tab2s, tab2_scales, 1)
         load_list("offs2")
-        load_weight(w3raw, w3, 0, 0, 256)
+        load_weight(w3raw[:, 0:1024], w3, 0, 0, 256)
         load_words(tab2w, tab2_words[0])
+        load_list("offs")
         load_page(0)
         nc.sync.dma_start(wgn[1][:], wg2)
         load_list("offs4")
@@ -211,44 +215,52 @@ def tile_list_annuity_slot_features_kernel(
         nc.vector.tensor_copy(v2s[:], tab2s[:].indirect(idx2[:]))
         weave(nc.vector.tensor_copy, w3st[:, 0:1024], w3raw[:, 0:1024], False)
         quantize(w3q[0][:, 0:256], w3s[0][:, 0:256], w3st[:, 0:1024])
-        nc.vector.tensor_copy(v2w[:], tab2w[:].bitcast(U32).indirect(idx2[:]))
-        stream2(0, h2[0][:], h2[0][:])
-        put(0, 0, 1)
-        stream2(1, h2[1][:], h2[1][:])
+        for half in range(2):
+            cols = slice(256 * half, 256 * (half + 1))
+            nc.vector.tensor_copy(v2w[:, cols], tab2w[:].bitcast(U32).indirect(idx2[:, 16 * half : 16 * (half + 1)]))
+            nc.tensor.matmul_mx(
+                banks[1][:, 0:256], lhsT=w3q[0][:, 0:P].bitcast(FP8X4), lhsT_scale=w3s[0][:, 0:P],
+                rhs=v2w[:, cols].bitcast(FP8X4), rhs_scale=v2s[:, cols], start=True, stop=True,
+            )
+            nc.scalar.activation(h2[0][:, cols], banks[1][:, 0:256], ACT.Tanh)
+            nc.scalar.activation(h2[0][:, cols], h2[0][:, cols], ACT.Exp)
+        nc.vector.tensor_copy(vs[:], tabs[:].indirect(idx[:]))
+        for half in range(2):
+            cols = slice(256 * half, 256 * (half + 1))
+            nc.vector.tensor_tensor(
+                pages[0][:].indirect(idx4[:, 16 * half : 16 * (half + 1)]), h2[0][:, cols], wgn[1][:, cols], ALU.mult,
+            )
+        stream2(1, banks[1], h2[1][:], h2[1][:])
 
-        load_weight(w3raw, w3, 0, 256, 256)
+        load_weight(w3raw[:, 1024:2048], w3, 0, 256, 256)
         load_page(1)
-        load_list("offs")
-        load_scale_rows(tabs, tab_scales, 2)
+        load_words(tabw[0], tab_words[0])
         for a in range(2):
-            load_weight(w1raw[a], w1, a, 0, 256)
-        for a in range(2):
-            load_words(tabw[a], tab_words[a])
+            load_weight(pair_raw[0][a], w1, a, 0, 256)
+        load_words(tabw[1], tab_words[1])
         load_page(2)
-        load_scale_rows(w2s, w2_scales, 2)
         load_w2(w2lo[0], 0, 256)
         load_page(3)
         nc.sync.dma_start(wgn[0][:], wg1)
         load_list("offs3")
         for a in range(2):
-            load_weight(w1raw[a], w1, a, 256, 256)
+            load_weight(pair_raw[1][a], w1, a, 256, 256)
         load_w2(w2lo[1], 256, 256)
         load_list("offs5")
 
         weave(nc.scalar.copy, w3st[:, 1024:2048], w3raw[:, 1024:2048], False)
         quantize(w3q[0][:, 256:512], w3s[0][:, 256:512], w3st[:, 1024:2048])
-        stream2(2, h2[2][:], h2[2][:])
-        stream2(3, h2[3][:], h2[3][:])
         put(1, 1, 1)
 
         def low_pair(u, slot):
             staged = slot[:].bitcast(BF16)
             for a in range(2):
-                weave(nc.scalar.copy, staged[:, 1024 * a : 1024 * (a + 1)], w1raw[a][:, 1024 * u : 1024 * (u + 1)], False)
+                weave(nc.scalar.copy, staged[:, 1024 * a : 1024 * (a + 1)], pair_raw[u][a], False)
             quantize(w1q[0][:, 512 * u : 512 * (u + 1)], w1s[0][:, 512 * u : 512 * (u + 1)], staged)
 
-        nc.vector.tensor_copy(vs[:], tabs[:].indirect(idx[:]))
         low_pair(0, slots[1])
+        stream2(2, banks[0], h2[2][:], h2[2][:])
+        stream2(3, banks[0], h2[3][:], h2[3][:])
         for a in range(2):
             nc.vector.tensor_copy(vw[a][:], tabw[a][:].bitcast(U32).indirect(idx[:]))
         for s in range(2):
@@ -265,15 +277,15 @@ def tile_list_annuity_slot_features_kernel(
             linear_low(s)
             stream1(s, s)
 
+        load_weight(w3raw[:], w3, 0, 512, 512)
+        for a in (1, 0):
+            load_weight(w1raw[a][:], w1, a, 512, 512)
+        load_w2(w2hi, 512, 512)
         with nc.allow_non_contiguous_dma(reason="one value a partition"):
             for dst, src in ((midc, mid), (gnc, gn)):
                 nc.sync.dma_start(dst[0][:], src[0:512].rearrange("(s p) -> p s", p=P))
                 nc.sync.dma_start(dst[1][:], src[512:1024].rearrange("(p i) -> p i", i=4))
-        load_weight(w3raw, w3, 0, 512, 512)
-        load_w2(w2hi, 512, 512)
         load_dealt_gates(wgp[1], wg2)
-        for a in (1, 0):
-            load_weight(w1raw[a], w1, a, 512, 512)
         load_page(4 + PLANE_ORDER[0])
         load_dealt_gates(wgp[0], wg1)
         load_page(4 + PLANE_ORDER[1])
@@ -301,7 +313,7 @@ def tile_list_annuity_slot_features_kernel(
         linear_high()
         h2_high = [w1raw[0][:, S * step : S * (step + 1)] for step in range(4)]
         for step, s in enumerate(PLANE_ORDER):
-            stream2(4 + s, h2_high[step], h2_high[step] if step < 3 else None)
+            stream2(4 + s, banks[3 - step % 2], h2_high[step], h2_high[step] if step < 3 else None)
             stream1(4 + s, step)
         fetch(2, slots[2][:])
         fetch(3, slots[3][:])
@@ -373,12 +385,28 @@ def tile_list_annuity_slot_features_kernel(
         for c in range(4):
             last_product(0, c)
         s = PLANE_ORDER[3]
-        for c in range(4):
+
+        def fetch_chunk(c):
             cols = slice(CHUNK * c, CHUNK * (c + 1))
-            got = slots[0][:, CHUNK * (c % 2) : CHUNK * (c % 2 + 1)]
-            nc.vector.tensor_copy(got, pages[4 + s][:].indirect(idx5[:, 16 * c : 16 * (c + 1)]))
+            nc.vector.tensor_copy(slots[0][:, cols], pages[4 + s][:].indirect(idx5[:, 16 * c : 16 * (c + 1)]))
+
+        def round_chunk(c):
+            cols = slice(CHUNK * c, CHUNK * (c + 1))
             nc.vector.tensor_scalar(
-                woven[:, cols, s], got, midc[1][:, s : s + 1], gnc[1][:, s : s + 1], ALU.subtract, ALU.mult,
+                woven[:, cols, s], slots[0][:, cols], midc[1][:, s : s + 1], gnc[1][:, s : s + 1], ALU.subtract, ALU.mult,
             )
+
+        def finish_chunk(c):
+            cols = slice(CHUNK * c, CHUNK * (c + 1))
             quantize(xq[1][:, cols], xs[1][:, cols], xb[:, 4 * CHUNK * c : 4 * CHUNK * (c + 1)])
             last_product(1, c)
+
+        fetch_chunk(0)
+        fetch_chunk(1)
+        round_chunk(0)
+        for c in range(4):
+            if c < 3:
+                round_chunk(c + 1)
+            finish_chunk(c)
+            if c < 2:
+                fetch_chunk(c + 2)

@@ -19,7 +19,7 @@ ALU = mybir.AluOpType
 
 P = 128
 CHUNK = 256
-PLANE_ORDER = (2, 0, 1, 3)
+PLANE_ORDER = (0, 3, 2, 1)
 
 
 def tile_list_annuity_slot_features_kernel(
@@ -56,8 +56,9 @@ def tile_list_annuity_slot_features_kernel(
         w1raw = [sb("w1raw%d" % a, [P, 2048], F32) for a in range(2)]
         w3raw = sb("w3raw", [P, 2048], F32)
         w3st = sb("w3st", [P, 2048], BF16)
+        twin = sb("twin", [P, 2 * PICKS], F32)
         joint = sb("joint", [P, PICKS + S], F32)
-        slots = [joint[:, 0:PICKS]] + [sb("slot%d" % s, [P, PICKS], F32)[:] for s in range(1, 4)]
+        slots = [joint[:, 0:PICKS]] + [sb("slot1", [P, PICKS], F32)[:], twin[:, 0:PICKS], twin[:, PICKS:]]
         w1q = [sb("w1q%d" % b, [P, 1024], U32) for b in range(2)]
         w1s = [sb("w1s%d" % b, [P, 1024], U8) for b in range(2)]
         w3q = [sb("w3q%d" % b, [P, 512], U32) for b in range(2)]
@@ -85,9 +86,9 @@ def tile_list_annuity_slot_features_kernel(
         ident = sb("ident", [P, P], F32)
         identb = sb("identb", [P, P], BF16)
 
-        def load_scale_rows(queue, dst, src, passes):
+        def load_scale_rows(dst, src, passes):
             for q in range(4):
-                queue.dma_start(
+                nc.sync.dma_start(
                     dst[32 * q : 32 * q + 4 * passes, :].bitcast(I32),
                     src[:, 4 * q : 4 * q + 4, :].bitcast(I32),
                 )
@@ -113,8 +114,8 @@ def tile_list_annuity_slot_features_kernel(
             src = w2_words.rearrange("a p c i -> p a (c i)")[:, :, 4 * c0 : 4 * (c0 + width)]
             nc.sync.dma_start(dst[:], src.bitcast(I32))
 
-        def load_dealt_gates(dst, wg):
-            for q in range(4):
+        def load_dealt_gates(dst, wg, quadrants):
+            for q in quadrants:
                 nc.sync.dma_start(dst[32 * q : 32 * (q + 1), :, :], wg.rearrange("(u i) s -> u i s", i=4))
 
         def weave(copy, dst, src, dealt):
@@ -134,8 +135,7 @@ def tile_list_annuity_slot_features_kernel(
                 rhs=v2w[:].bitcast(FP8X4), rhs_scale=v2s[:], start=True, stop=True,
             )
             nc.scalar.activation(bent, bank[:], ACT.Tanh)
-            if dst is not None:
-                nc.scalar.activation(dst, bent, ACT.Exp)
+            nc.scalar.activation(dst, bent, ACT.Exp)
 
         def picked(a, jb):
             cols = slice(P * jb, P * (jb + 1))
@@ -164,7 +164,7 @@ def tile_list_annuity_slot_features_kernel(
                     bank[:].rearrange("p (m i) -> p i m", i=4),
                 )
 
-        def stream1(t, step):
+        def stream1(t, step, dst):
             b, s = divmod(t, 4)
             bank = banks[2 + (step + b) % 2]
             for jb in range(4):
@@ -182,8 +182,8 @@ def tile_list_annuity_slot_features_kernel(
                 cols = slice(P * jb, P * (jb + 1))
                 nc.tensor.matmul(total[:, cols], lhsT=lin[:, cols], rhs=ident[:], is_transpose=True, start=True, stop=False)
                 nc.tensor.matmul(total[:, cols], lhsT=bent[:, cols], rhs=ident[:], is_transpose=True, start=False, stop=True)
-            if t not in (1, 7):
-                nc.scalar.copy(h1[step % 4][:], total[:])
+            if dst is not None:
+                nc.scalar.copy(dst, total[:])
 
         def put(t, step, which, values=None):
             b, s = divmod(t, 4)
@@ -195,15 +195,14 @@ def tile_list_annuity_slot_features_kernel(
         def fetch(t, slot):
             nc.vector.tensor_copy(slot, pages[t][:].indirect(idx5[:]))
 
-        for plane in (tab2s, tabs, w2s):
+        nc.gpsimd.memset(tab2s[:].bitcast(I32), 0)
+        for plane in (tabs, w2s):
             nc.vector.memset(plane[:].bitcast(I32), 0)
         nc.vector.memset(w4s[:].rearrange("p a c -> p (a c)").bitcast(I32), 0)
-        load_scale_rows(nc.gpsimd, tabs, tab_scales, 2)
-        load_scale_rows(nc.gpsimd, w2s, w2_scales, 2)
         make_identity(nc, ident[:])
         make_identity(nc, identb[:])
 
-        load_scale_rows(nc.sync, tab2s, tab2_scales, 1)
+        load_scale_rows(tab2s, tab2_scales, 1)
         load_list("offs2")
         load_weight(w3raw[:, 0:1024], w3, 0, 0, 256)
         load_words(tab2w, tab2_words[0])
@@ -224,7 +223,6 @@ def tile_list_annuity_slot_features_kernel(
             )
             nc.scalar.activation(h2[0][:, cols], banks[1][:, 0:256], ACT.Tanh)
             nc.scalar.activation(h2[0][:, cols], h2[0][:, cols], ACT.Exp)
-        nc.vector.tensor_copy(vs[:], tabs[:].indirect(idx[:]))
         for half in range(2):
             cols = slice(256 * half, 256 * (half + 1))
             nc.vector.tensor_tensor(
@@ -234,11 +232,13 @@ def tile_list_annuity_slot_features_kernel(
 
         load_weight(w3raw[:, 1024:2048], w3, 0, 256, 256)
         load_page(1)
+        load_scale_rows(tabs, tab_scales, 2)
         load_words(tabw[0], tab_words[0])
         for a in range(2):
             load_weight(pair_raw[0][a], w1, a, 0, 256)
         load_words(tabw[1], tab_words[1])
         load_page(2)
+        load_scale_rows(w2s, w2_scales, 2)
         load_w2(w2lo[0], 0, 256)
         load_page(3)
         nc.sync.dma_start(wgn[0][:], wg1)
@@ -252,51 +252,50 @@ def tile_list_annuity_slot_features_kernel(
         quantize(w3q[0][:, 256:512], w3s[0][:, 256:512], w3st[:, 1024:2048])
         put(1, 1, 1)
 
-        def low_pair(u, slot):
+        def low_pair(u, slot, copy):
             staged = slot[:].bitcast(BF16)
             for a in range(2):
-                weave(nc.scalar.copy, staged[:, 1024 * a : 1024 * (a + 1)], pair_raw[u][a], False)
+                weave(copy, staged[:, 1024 * a : 1024 * (a + 1)], pair_raw[u][a], False)
             quantize(w1q[0][:, 512 * u : 512 * (u + 1)], w1s[0][:, 512 * u : 512 * (u + 1)], staged)
 
-        low_pair(0, slots[1])
+        nc.vector.tensor_copy(vs[:], tabs[:].indirect(idx[:]))
+        low_pair(0, slots[1], nc.vector.tensor_copy)
         stream2(2, banks[0], h2[2][:], h2[2][:])
         stream2(3, banks[0], h2[3][:], h2[3][:])
         for a in range(2):
             nc.vector.tensor_copy(vw[a][:], tabw[a][:].bitcast(U32).indirect(idx[:]))
         for s in range(2):
             linear_low(s)
-            stream1(s, s)
+            stream1(s, s, h1[0] if s == 0 else None)
         put(2, 2, 1)
         put(3, 3, 1)
-        low_pair(1, joint[:, S:])
+        low_pair(1, joint[:, S:], nc.scalar.copy)
         nc.scalar.copy(h1[1], banks[7][:])
         put(0, 0, 0)
         fetch(0, slots[0][:])
         put(1, 1, 0)
         for s in range(2, 4):
             linear_low(s)
-            stream1(s, s)
+            stream1(s, s, h1[s])
 
         load_weight(w3raw[:], w3, 0, 512, 512)
         for a in (1, 0):
             load_weight(w1raw[a][:], w1, a, 512, 512)
         load_w2(w2hi, 512, 512)
+        load_dealt_gates(wgp[1], wg2, range(4))
         with nc.allow_non_contiguous_dma(reason="one value a partition"):
             for dst, src in ((midc, mid), (gnc, gn)):
                 nc.sync.dma_start(dst[0][:], src[0:512].rearrange("(s p) -> p s", p=P))
                 nc.sync.dma_start(dst[1][:], src[512:1024].rearrange("(p i) -> p i", i=4))
-        load_dealt_gates(wgp[1], wg2)
-        load_page(4 + PLANE_ORDER[0])
-        load_dealt_gates(wgp[0], wg1)
-        load_page(4 + PLANE_ORDER[1])
+        for s in PLANE_ORDER:
+            load_page(4 + s)
+        load_dealt_gates(wgp[0], wg1, range(4))
         for q in range(4):
             nc.sync.dma_start(
                 w4s[32 * q : 32 * q + 4, :, :].bitcast(I32),
                 w4_scales[:, 4 * q : 4 * q + 4, :].rearrange("a r c -> r a c").bitcast(I32),
             )
         nc.sync.dma_start(w4w[:].bitcast(I32), w4_words.rearrange("a p c -> p a c").bitcast(I32))
-        for s in PLANE_ORDER[2:]:
-            load_page(4 + s)
 
         fetch(1, slots[1][:])
         for b in range(2):
@@ -308,13 +307,14 @@ def tile_list_annuity_slot_features_kernel(
             weave(nc.scalar.copy, slots[2 + a][:].bitcast(BF16), w1raw[a][:], True)
         put(2, 2, 0)
         put(3, 3, 0)
-        for a in (1, 0):
-            quantize(w1q[1][:, 512 * a : 512 * (a + 1)], w1s[1][:, 512 * a : 512 * (a + 1)], slots[2 + a][:].bitcast(BF16))
+        quantize(w1q[1][:], w1s[1][:], twin[:].bitcast(BF16))
         linear_high()
+        h1_high = [h1[0], lin1[:, 1536:2048], h1[2], None]
         h2_high = [w1raw[0][:, S * step : S * (step + 1)] for step in range(4)]
         for step, s in enumerate(PLANE_ORDER):
-            stream2(4 + s, banks[3 - step % 2], h2_high[step], h2_high[step] if step < 3 else None)
-            stream1(4 + s, step)
+            stream2(4 + s, banks[5], h2_high[step], h2_high[step])
+        for step, s in enumerate(PLANE_ORDER):
+            stream1(4 + s, step, h1_high[step])
         fetch(2, slots[2][:])
         fetch(3, slots[3][:])
 
@@ -324,6 +324,11 @@ def tile_list_annuity_slot_features_kernel(
                 xb[:, PICKS * s : PICKS * (s + 1)], slots[s][:], ACT.Identity,
                 bias=shift[0][:, s : s + 1], scale=gnc[0][:, s : s + 1],
             )
+        for step, s in enumerate(PLANE_ORDER):
+            put(4 + s, step, 1, h2_high[step])
+        for step, s in enumerate(PLANE_ORDER[:2]):
+            put(4 + s, step, 0, h1_high[step])
+            fetch(4 + s, slots[step][:])
         for g in range(4):
             turned = banks[g % 2][:].bitcast(BF16)
             for jj in range(2):
@@ -343,21 +348,20 @@ def tile_list_annuity_slot_features_kernel(
             )
 
         woven = xb.rearrange("p (j i) -> p j i", i=4)
-        for step, s in enumerate(PLANE_ORDER[:3]):
-            put(4 + s, step, 1, h2_high[step])
-            put(4 + s, step, 0)
-            slot = slots[step][:]
-            if step == 2:
-                quantize(xq[0][:], xs[0][:], lin1[:].bitcast(BF16))
-                slot = lin1[:, 0:PICKS]
-                nc.scalar.activation(lin1[:, 1024:1536], h2_high[3], ACT.Exp)
-                nc.scalar.copy(lin1[:, 1536:2048], banks[7][:])
-            fetch(4 + s, slot)
+
+        def round_plane(s, got):
             nc.scalar.activation(
-                woven[:, :, s], slot, ACT.Identity,
-                bias=shift[1][:, s : s + 1], scale=gnc[1][:, s : s + 1],
+                woven[:, :, s], got, ACT.Identity, bias=shift[1][:, s : s + 1], scale=gnc[1][:, s : s + 1],
             )
-        put(4 + PLANE_ORDER[3], 3, 1, lin1[:, 1024:1536])
+
+        for step, s in enumerate(PLANE_ORDER[:2]):
+            round_plane(s, slots[step][:])
+        s = PLANE_ORDER[2]
+        put(4 + s, 2, 0, h1_high[2])
+        quantize(xq[0][:], xs[0][:], lin1[:].bitcast(BF16))
+        nc.scalar.copy(lin1[:, 1536:2048], banks[7][:])
+        fetch(4 + s, lin1[:, 0:PICKS])
+        round_plane(s, lin1[:, 0:PICKS])
         put(4 + PLANE_ORDER[3], 3, 0, lin1[:, 1536:2048])
 
         def last_product(b, c):
@@ -387,13 +391,13 @@ def tile_list_annuity_slot_features_kernel(
         s = PLANE_ORDER[3]
 
         def fetch_chunk(c):
-            cols = slice(CHUNK * c, CHUNK * (c + 1))
+            cols = slice(CHUNK * (c % 2), CHUNK * (c % 2 + 1))
             nc.vector.tensor_copy(slots[0][:, cols], pages[4 + s][:].indirect(idx5[:, 16 * c : 16 * (c + 1)]))
 
         def round_chunk(c):
             cols = slice(CHUNK * c, CHUNK * (c + 1))
             nc.vector.tensor_scalar(
-                woven[:, cols, s], slots[0][:, cols], midc[1][:, s : s + 1], gnc[1][:, s : s + 1], ALU.subtract, ALU.mult,
+                woven[:, cols, s], slots[0][:, CHUNK * (c % 2) : CHUNK * (c % 2 + 1)], midc[1][:, s : s + 1], gnc[1][:, s : s + 1], ALU.subtract, ALU.mult,
             )
 
         def finish_chunk(c):

from contextlib import ExitStack

import concourse.mybir as mybir
from concourse.masks import make_identity

K, K2, T, T3, S, H, T2, PICKS, N = 1024, 512, 2048, 1024, 512, 1024, 2048, 1024, 512
FLOPS = 2 * (2 * K * H * S + K2 * H * S + H * N * PICKS)

F32 = mybir.dt.float32
BF16 = mybir.dt.bfloat16
I32 = mybir.dt.int32
U32 = mybir.dt.uint32
U16 = mybir.dt.uint16
U8 = mybir.dt.uint8
FP8X4 = mybir.dt.float8_e4m3fn_x4
FP4X4 = mybir.dt.float4_e2m1fn_x4
ACT = mybir.ActivationFunctionType
ALU = mybir.AluOpType

P = 128
CHUNK = 256
PLANE_ORDER = (0, 3, 2, 1)


def tile_list_annuity_slot_features_kernel(
    tc, tab_words, tab_scales, tab2_words, tab2_scales, offs, offs2, offs3, offs4, offs5,
    w1, w2_words, w2_scales, w3, w4_words, w4_scales, wg1, wg2, page0, mid, gn, out,
):
    nc = tc.nc
    with ExitStack() as ctx:
        keep = ctx.enter_context(tc.tile_pool(name="keep", bufs=1))
        psum = ctx.enter_context(tc.psum_pool(name="psum", bufs=1))

        def sb(name, shape, dtype):
            return keep.tile(shape, dtype, name=name, align_bytes=64)

        lists = {}
        for name, src in (("offs", offs), ("offs2", offs2), ("offs3", offs3), ("offs4", offs4), ("offs5", offs5)):
            lists[name] = (keep.tile(list(src.shape), U16, name="l_" + name), src)

        def load_list(name):
            nc.sync.dma_start(lists[name][0][:], lists[name][1])

        idx, idx2, idx3, idx4, idx5 = (lists[n][0] for n in ("offs", "offs2", "offs3", "offs4", "offs5"))

        banks = [psum.tile([P, 512], F32, name="bank%d" % b) for b in range(8)]
        pages = [sb("page%d" % t, [P, T2], F32) for t in range(8)]
        tabw = [sb("tabw%d" % a, [P, T], I32) for a in range(2)]
        tabs = sb("tabs", [P, T], U8)
        tab2w = sb("tab2w", [P, T3], I32)
        tab2s = sb("tab2s", [P, T3], U8)
        vw = [sb("vw%d" % a, [P, S], U32) for a in range(2)]
        vs = sb("vs", [P, S], U8)
        v2w = sb("v2w", [P, S], U32)
        v2s = sb("v2s", [P, S], U8)
        w1raw = [sb("w1raw%d" % a, [P, 2048], F32) for a in range(2)]
        w3raw = sb("w3raw", [P, 2048], F32)
        w3st = sb("w3st", [P, 2048], BF16)
        twin = sb("twin", [P, 2 * PICKS], F32)
        joint = sb("joint", [P, PICKS + S], F32)
        slots = [joint[:, 0:PICKS]] + [sb("slot1", [P, PICKS], F32)[:], twin[:, 0:PICKS], twin[:, PICKS:]]
        w1q = [sb("w1q%d" % b, [P, 1024], U32) for b in range(2)]
        w1s = [sb("w1s%d" % b, [P, 1024], U8) for b in range(2)]
        w3q = [sb("w3q%d" % b, [P, 512], U32) for b in range(2)]
        w3s = [sb("w3s%d" % b, [P, 512], U8) for b in range(2)]
        w2lo = [sb("w2lo%d" % u, [P, 2, 256], I32) for u in range(2)]
        w2hi = sb("w2hi", [P, 2, 512], I32)
        w2s = sb("w2s", [P, H], U8)
        w4w = sb("w4w", [P, 2, 2 * N], U8)
        w4s = sb("w4s", [P, 2, N], U8)
        wgn = [sb("wgn%d" % i, [P, S], F32) for i in range(2)]
        wgp = [sb("wgp%d" % i, [P, 4, S], F32) for i in range(2)]
        h1 = [joint[:, PICKS:] if s == 1 else sb("h1_%d" % s, [P, S], F32)[:] for s in range(4)]
        pair_raw = [
            [wgp[1 - u][:].rearrange("p i s -> p (i s)")[:, 1024 * a : 1024 * (a + 1)] for a in range(2)] for u in range(2)
        ]
        h2 = [sb("h2_%d" % s, [P, S], F32) for s in range(4)]
        tanh_t = [sb("tanh%d" % s, [P, 512], F32) for s in range(2)]
        lin_t = [sb("lin%d" % s, [P, 512], F32) for s in range(2)]
        lin1 = sb("lin_hi", [P, 2048], F32)
        xq = [sb("xq%d" % b, [P, PICKS], U32) for b in range(2)]
        xs = [sb("xs%d" % b, [P, PICKS], U8) for b in range(2)]
        midc = [sb("mid%d" % b, [P, 4], F32) for b in range(2)]
        gnc = [sb("gn%d" % b, [P, 4], F32) for b in range(2)]
        shift = [sb("shift%d" % b, [P, 4], F32) for b in range(2)]
        ident = sb("ident", [P, P], F32)
        identb = sb("identb", [P, P], BF16)

        def load_scale_rows(dst, src, passes):
            for q in range(4):
                nc.sync.dma_start(
                    dst[32 * q : 32 * q + 4 * passes, :].bitcast(I32),
                    src[:, 4 * q : 4 * q + 4, :].bitcast(I32),
                )

        def load_words(dst, src):
            nc.sync.dma_start(dst[:], src.rearrange("p t i -> p (t i)").bitcast(I32))

        def load_page(t):
            b, s = divmod(t, 4)
            rows = page0[512 * b : 512 * (b + 1), :]
            if b == 0:
                nc.sync.dma_start(pages[t][:], rows[P * s : P * (s + 1), :])
            else:
                nc.sync.dma_start(pages[t][:], rows.rearrange("(p i) c -> p i c", i=4)[:, s, :])

        def load_weight(raw, w, a, c0, width):
            nc.sync.dma_start(
                raw.rearrange("p (j c) -> p j c", j=4),
                w[512 * a : 512 * (a + 1), c0 : c0 + width].rearrange("(p j) c -> p j c", j=4),
            )

        def load_w2(dst, c0, width):
            src = w2_words.rearrange("a p c i -> p a (c i)")[:, :, 4 * c0 : 4 * (c0 + width)]
            nc.sync.dma_start(dst[:], src.bitcast(I32))

        def load_dealt_gates(dst, wg, quadrants):
            for q in quadrants:
                nc.sync.dma_start(dst[32 * q : 32 * (q + 1), :, :], wg.rearrange("(u i) s -> u i s", i=4))

        def weave(copy, dst, src, dealt):
            if dealt:
                copy(dst.rearrange("p (t m j) -> p m j t", t=4, j=4), src.rearrange("p (j m t) -> p m j t", j=4, t=4))
            else:
                copy(dst.rearrange("p (c i j) -> p c j i", i=4, j=4), src.rearrange("p (j c i) -> p c j i", j=4, i=4))

        def quantize(codes, scales, src):
            nc.vector.quantize_mx(out=codes.bitcast(FP8X4), scales=scales, in_=src)

        def stream2(t, bank, bent, dst):
            b, s = divmod(t, 4)
            cols = slice(P * s, P * (s + 1))
            nc.tensor.matmul_mx(
                bank[:], lhsT=w3q[b][:, cols].bitcast(FP8X4), lhsT_scale=w3s[b][:, cols],
                rhs=v2w[:].bitcast(FP8X4), rhs_scale=v2s[:], start=True, stop=True,
            )
            nc.scalar.activation(bent, bank[:], ACT.Tanh)
            nc.scalar.activation(dst, bent, ACT.Exp)

        def picked(a, jb):
            cols = slice(P * jb, P * (jb + 1))
            return dict(lhsT=vw[a][:, cols].bitcast(FP8X4), lhsT_scale=vs[4 * a : P, cols])

        def linear_low(s):
            bank = banks[4 + s % 2]
            for jb in range(4):
                for a in range(2):
                    nc.tensor.matmul_mx(
                        bank[:, P * jb : P * (jb + 1)], rhs=w2lo[s // 2][:, a, P * (s % 2) : P * (s % 2 + 1)].bitcast(FP8X4),
                        rhs_scale=w2s[4 * a : P, P * s : P * (s + 1)], start=(a == 0), stop=(a == 1), **picked(a, jb),
                    )
            nc.scalar.copy(lin_t[s % 2][:], bank[:])

        def linear_high():
            for jb in range(4):
                bank = banks[4 + jb % 2]
                for a in range(2):
                    nc.tensor.matmul_mx(
                        bank[:], rhs=w2hi[:, a, :].bitcast(FP8X4), rhs_scale=w2s[4 * a : P, 512:1024],
                        start=(a == 0), stop=(a == 1), **picked(a, jb),
                    )
                nc.scalar.copy(
                    lin1[:].rearrange("p (i b m) -> p b i m", i=4, b=4)[:, jb, :, :],
                    bank[:].rearrange("p (m i) -> p i m", i=4),
                )

        def stream1(t, step, dst):
            b, s = divmod(t, 4)
            bank = banks[2 + (step + b) % 2]
            for jb in range(4):
                for a in range(2):
                    c0 = 512 * (s // 2) + 256 * a + P * (s % 2) if b == 0 else 512 * a + P * s
                    nc.tensor.matmul_mx(
                        bank[:, P * jb : P * (jb + 1)], rhs=w1q[b][:, c0 : c0 + P].bitcast(FP8X4),
                        rhs_scale=w1s[b][:, c0 : c0 + P], start=(a == 0), stop=(a == 1), **picked(a, jb),
                    )
            bent = tanh_t[step % 2]
            nc.scalar.activation(bent[:], bank[:], ACT.Tanh)
            lin = lin_t[s % 2][:] if b == 0 else lin1[:, 512 * s : 512 * (s + 1)]
            total = banks[6 + step % 2]
            for jb in range(4):
                cols = slice(P * jb, P * (jb + 1))
                nc.tensor.matmul(total[:, cols], lhsT=lin[:, cols], rhs=ident[:], is_transpose=True, start=True, stop=False)
                nc.tensor.matmul(total[:, cols], lhsT=bent[:, cols], rhs=ident[:], is_transpose=True, start=False, stop=True)
            if dst is not None:
                nc.scalar.copy(dst, total[:])

        def put(t, step, which, values=None):
            b, s = divmod(t, 4)
            gate = wgn[which][:] if b == 0 else wgp[which][:, s, :]
            if values is None:
                values = (h1, h2)[which][step % 4][:]
            nc.vector.tensor_tensor(pages[t][:].indirect((idx3, idx4)[which][:]), values, gate, ALU.mult)

        def fetch(t, slot):
            nc.vector.tensor_copy(slot, pages[t][:].indirect(idx5[:]))

        nc.gpsimd.memset(tab2s[:].bitcast(I32), 0)
        for plane in (tabs, w2s):
            nc.vector.memset(plane[:].bitcast(I32), 0)
        nc.vector.memset(w4s[:].rearrange("p a c -> p (a c)").bitcast(I32), 0)
        make_identity(nc, ident[:])
        make_identity(nc, identb[:])

        load_scale_rows(tab2s, tab2_scales, 1)
        load_list("offs2")
        load_weight(w3raw[:, 0:1024], w3, 0, 0, 256)
        load_words(tab2w, tab2_words[0])
        load_list("offs")
        load_page(0)
        nc.sync.dma_start(wgn[1][:], wg2)
        load_list("offs4")

        nc.vector.tensor_copy(v2s[:], tab2s[:].indirect(idx2[:]))
        weave(nc.vector.tensor_copy, w3st[:, 0:1024], w3raw[:, 0:1024], False)
        quantize(w3q[0][:, 0:256], w3s[0][:, 0:256], w3st[:, 0:1024])
        for half in range(2):
            cols = slice(256 * half, 256 * (half + 1))
            nc.vector.tensor_copy(v2w[:, cols], tab2w[:].bitcast(U32).indirect(idx2[:, 16 * half : 16 * (half + 1)]))
            nc.tensor.matmul_mx(
                banks[1][:, 0:256], lhsT=w3q[0][:, 0:P].bitcast(FP8X4), lhsT_scale=w3s[0][:, 0:P],
                rhs=v2w[:, cols].bitcast(FP8X4), rhs_scale=v2s[:, cols], start=True, stop=True,
            )
            nc.scalar.activation(h2[0][:, cols], banks[1][:, 0:256], ACT.Tanh)
            nc.scalar.activation(h2[0][:, cols], h2[0][:, cols], ACT.Exp)
        for half in range(2):
            cols = slice(256 * half, 256 * (half + 1))
            nc.vector.tensor_tensor(
                pages[0][:].indirect(idx4[:, 16 * half : 16 * (half + 1)]), h2[0][:, cols], wgn[1][:, cols], ALU.mult,
            )
        stream2(1, banks[1], h2[1][:], h2[1][:])

        load_weight(w3raw[:, 1024:2048], w3, 0, 256, 256)
        load_page(1)
        load_scale_rows(tabs, tab_scales, 2)
        load_words(tabw[0], tab_words[0])
        for a in range(2):
            load_weight(pair_raw[0][a], w1, a, 0, 256)
        load_words(tabw[1], tab_words[1])
        load_page(2)
        load_scale_rows(w2s, w2_scales, 2)
        load_w2(w2lo[0], 0, 256)
        load_page(3)
        nc.sync.dma_start(wgn[0][:], wg1)
        load_list("offs3")
        for a in range(2):
            load_weight(pair_raw[1][a], w1, a, 256, 256)
        load_w2(w2lo[1], 256, 256)
        load_list("offs5")

        weave(nc.scalar.copy, w3st[:, 1024:2048], w3raw[:, 1024:2048], False)
        quantize(w3q[0][:, 256:512], w3s[0][:, 256:512], w3st[:, 1024:2048])
        put(1, 1, 1)

        def low_pair(u, slot, copy):
            staged = slot[:].bitcast(BF16)
            for a in range(2):
                weave(copy, staged[:, 1024 * a : 1024 * (a + 1)], pair_raw[u][a], False)
            quantize(w1q[0][:, 512 * u : 512 * (u + 1)], w1s[0][:, 512 * u : 512 * (u + 1)], staged)

        nc.vector.tensor_copy(vs[:], tabs[:].indirect(idx[:]))
        low_pair(0, slots[1], nc.vector.tensor_copy)
        stream2(2, banks[0], h2[2][:], h2[2][:])
        stream2(3, banks[0], h2[3][:], h2[3][:])
        for a in range(2):
            nc.vector.tensor_copy(vw[a][:], tabw[a][:].bitcast(U32).indirect(idx[:]))
        for s in range(2):
            linear_low(s)
            stream1(s, s, h1[0] if s == 0 else None)
        put(2, 2, 1)
        put(3, 3, 1)
        low_pair(1, joint[:, S:], nc.scalar.copy)
        nc.scalar.copy(h1[1], banks[7][:])
        put(0, 0, 0)
        fetch(0, slots[0][:])
        put(1, 1, 0)
        for s in range(2, 4):
            linear_low(s)
            stream1(s, s, h1[s])

        load_weight(w3raw[:], w3, 0, 512, 512)
        for a in (1, 0):
            load_weight(w1raw[a][:], w1, a, 512, 512)
        load_w2(w2hi, 512, 512)
        load_dealt_gates(wgp[1], wg2, range(4))
        with nc.allow_non_contiguous_dma(reason="one value a partition"):
            for dst, src in ((midc, mid), (gnc, gn)):
                nc.sync.dma_start(dst[0][:], src[0:512].rearrange("(s p) -> p s", p=P))
                nc.sync.dma_start(dst[1][:], src[512:1024].rearrange("(p i) -> p i", i=4))
        for s in PLANE_ORDER:
            load_page(4 + s)
        load_dealt_gates(wgp[0], wg1, range(4))
        for q in range(4):
            nc.sync.dma_start(
                w4s[32 * q : 32 * q + 4, :, :].bitcast(I32),
                w4_scales[:, 4 * q : 4 * q + 4, :].rearrange("a r c -> r a c").bitcast(I32),
            )
        nc.sync.dma_start(w4w[:].bitcast(I32), w4_words.rearrange("a p c -> p a c").bitcast(I32))

        fetch(1, slots[1][:])
        for b in range(2):
            nc.vector.scalar_tensor_tensor(shift[b][:], midc[b][:], -1.0, gnc[b][:], ALU.mult, ALU.mult)

        weave(nc.scalar.copy, w3st[:], w3raw[:], True)
        quantize(w3q[1][:], w3s[1][:], w3st[:])
        for a in (1, 0):
            weave(nc.scalar.copy, slots[2 + a][:].bitcast(BF16), w1raw[a][:], True)
        put(2, 2, 0)
        put(3, 3, 0)
        quantize(w1q[1][:], w1s[1][:], twin[:].bitcast(BF16))
        linear_high()
        h1_high = [h1[0], lin1[:, 1536:2048], h1[2], None]
        h2_high = [w1raw[0][:, S * step : S * (step + 1)] for step in range(4)]
        for step, s in enumerate(PLANE_ORDER):
            stream2(4 + s, banks[5], h2_high[step], h2_high[step])
        for step, s in enumerate(PLANE_ORDER):
            stream1(4 + s, step, h1_high[step])
        fetch(2, slots[2][:])
        fetch(3, slots[3][:])

        xb = w1raw[1][:].bitcast(BF16)
        for s in range(4):
            nc.scalar.activation(
                xb[:, PICKS * s : PICKS * (s + 1)], slots[s][:], ACT.Identity,
                bias=shift[0][:, s : s + 1], scale=gnc[0][:, s : s + 1],
            )
        for step, s in enumerate(PLANE_ORDER):
            put(4 + s, step, 1, h2_high[step])
        for step, s in enumerate(PLANE_ORDER[:2]):
            put(4 + s, step, 0, h1_high[step])
            fetch(4 + s, slots[step][:])
        for g in range(4):
            turned = banks[g % 2][:].bitcast(BF16)
            for jj in range(2):
                for s in range(4):
                    j0 = PICKS * s + CHUNK * g + P * jj
                    nc.tensor.transpose(turned[:, 512 * jj + P * s : 512 * jj + P * (s + 1)], xb[:, j0 : j0 + P], identb[:])
            words = tanh_t[g % 2]
            nc.scalar.copy(words[:].bitcast(BF16), turned)
            back = banks[4 + g % 2]
            for jj in range(2):
                for u in range(2):
                    c0 = 256 * jj + P * u
                    nc.tensor.transpose(back[:, c0 : c0 + P], words[:, 256 * jj + u : 256 * (jj + 1) : 2], ident[:])
            nc.scalar.copy(
                lin1[:, 512 * g : 512 * (g + 1)].rearrange("p (b j u) -> p b j u", b=2, u=2),
                back[:].rearrange("p (b u j) -> p b j u", b=2, u=2),
            )

        woven = xb.rearrange("p (j i) -> p j i", i=4)

        def round_plane(s, got):
            nc.scalar.activation(
                woven[:, :, s], got, ACT.Identity, bias=shift[1][:, s : s + 1], scale=gnc[1][:, s : s + 1],
            )

        for step, s in enumerate(PLANE_ORDER[:2]):
            round_plane(s, slots[step][:])
        s = PLANE_ORDER[2]
        put(4 + s, 2, 0, h1_high[2])
        quantize(xq[0][:], xs[0][:], lin1[:].bitcast(BF16))
        nc.scalar.copy(lin1[:, 1536:2048], banks[7][:])
        fetch(4 + s, lin1[:, 0:PICKS])
        round_plane(s, lin1[:, 0:PICKS])
        put(4 + PLANE_ORDER[3], 3, 0, lin1[:, 1536:2048])

        def last_product(b, c):
            for half in range(2):
                bank = banks[2 * c + half]
                for nn in range(2):
                    nt = 2 * half + nn
                    for jj in range(2):
                        j0 = CHUNK * c + P * jj
                        nc.tensor.matmul_mx(
                            bank[:, CHUNK * nn + P * jj : CHUNK * nn + P * (jj + 1)],
                            lhsT=w4w[:, b, 2 * P * nt : 2 * P * (nt + 1)].bitcast(FP4X4),
                            lhsT_scale=w4s[:, b, P * nt : P * (nt + 1)],
                            rhs=xq[b][:, j0 : j0 + P].bitcast(FP8X4), rhs_scale=xs[b][:, j0 : j0 + P],
                            start=(b == 0 and nn == 0 and jj == 0), stop=(b == 1 and nn == 1 and jj == 1),
                        )
                if b == 1:
                    staged = (h2 + h1)[2 * c + half]
                    nc.scalar.activation(staged[:], bank[:], ACT.Square)
                    nc.sync.dma_start(
                        out.rearrange("(n p) j -> p n j", p=P)[:, 2 * half : 2 * half + 2, CHUNK * c : CHUNK * (c + 1)],
                        staged[:].rearrange("p (n j) -> p n j", n=2),
                    )

        for c in range(4):
            last_product(0, c)
        s = PLANE_ORDER[3]

        def fetch_chunk(c):
            cols = slice(CHUNK * (c % 2), CHUNK * (c % 2 + 1))
            nc.vector.tensor_copy(slots[0][:, cols], pages[4 + s][:].indirect(idx5[:, 16 * c : 16 * (c + 1)]))

        def round_chunk(c):
            cols = slice(CHUNK * c, CHUNK * (c + 1))
            nc.vector.tensor_scalar(
                woven[:, cols, s], slots[0][:, CHUNK * (c % 2) : CHUNK * (c % 2 + 1)], midc[1][:, s : s + 1], gnc[1][:, s : s + 1], ALU.subtract, ALU.mult,
            )

        def finish_chunk(c):
            cols = slice(CHUNK * c, CHUNK * (c + 1))
            quantize(xq[1][:, cols], xs[1][:, cols], xb[:, 4 * CHUNK * c : 4 * CHUNK * (c + 1)])
            last_product(1, c)

        fetch_chunk(0)
        fetch_chunk(1)
        round_chunk(0)
        for c in range(4):
            if c < 3:
                round_chunk(c + 1)
            finish_chunk(c)
            if c < 2:
                fetch_chunk(c + 2)
